import numpy as np
import ml_dtypes


def mxq(x, axis, fmt="e4m3"):
    dtype, down = {"e4m3": (ml_dtypes.float8_e4m3fn, 7), "e5m2": (ml_dtypes.float8_e5m2, 14)}[fmt]
    v = np.moveaxis(np.asarray(x, np.float32).astype(ml_dtypes.bfloat16).astype(np.float64), axis, -1)
    blocks = v.reshape(v.shape[:-1] + (-1, 32))
    amax = np.abs(blocks).max(-1, keepdims=True)
    byte = np.maximum(np.where(amax > 0, np.frexp(amax)[1] - 1 + 127, 0) - down, 1)
    scale = np.exp2(byte - 127.0)
    codes = (blocks / scale).astype(np.float32).astype(dtype).astype(np.float64)
    return np.moveaxis((codes * scale).reshape(v.shape), -1, axis)


WIDE = False


def mx_kscale(k):
    if not WIDE:
        return np.ones(k)
    levels = np.array([10, -10, 5, -5, 0])
    if k % 512:
        return np.exp2(np.random.permutation(np.resize(levels, k // 32))).repeat(32)
    a = np.empty((k // 512, 16))
    for p in range(k // 512):
        a[p, :8] = np.random.permutation(np.resize(levels, 8))
        for g in range(8):
            far = levels[np.abs(levels - a[p, g]) >= 10]
            a[p, g + 8] = far[np.random.randint(len(far))]
    return np.exp2(a.ravel()).repeat(32)


def f64(x):
    return np.asarray(x).astype(np.float64)


def striped(idx):
    return np.tile(np.asarray(idx).reshape(-1, 16).T, (8, 1)).astype(np.uint16)


def unstriped(offs):
    return offs[:16].T.reshape(-1).astype(np.int64)


E2M1 = np.array([0.0, 0.5, 1.0, 1.5, 2.0, 3.0, 4.0, 6.0, -0.0, -0.5, -1.0, -1.5, -2.0, -3.0, -4.0, -6.0])


def pack_weight(w, fmt):
    k, n = w.shape
    w = f64(np.asarray(w, np.float32).astype(ml_dtypes.bfloat16)).reshape(k // 32, 32, n)
    amax = np.abs(w).max(1)
    if fmt == "e4m3":
        byte = np.frexp(amax)[1] - 1 + 127 - 7
    else:
        mant, ex = np.frexp(amax / 6.0)
        byte = np.where(mant > 0.5, ex, ex - 1) + 127
    byte = np.clip(np.where(amax > 0, byte, 1), 1, 254)
    scaled = (w * np.exp2(127.0 - byte)[:, None, :]).reshape(k, n).astype(np.float32)
    by_word = np.ascontiguousarray(scaled.reshape(k // 512, 128, 4, n).transpose(0, 1, 3, 2))
    if fmt == "e4m3":
        words = by_word.astype(ml_dtypes.float8_e4m3fn).view(np.uint8)
    else:
        c = by_word.astype(ml_dtypes.float4_e2m1fn).view(np.uint8) & 0xF
        words = (c[..., 0::2] | (c[..., 1::2] << 4)).reshape(k // 512, 128, 2 * n)
    return np.ascontiguousarray(words), np.ascontiguousarray(byte.astype(np.uint8).reshape(k // 512, 16, n))


def unpack_weight(words, scales, fmt):
    g, _, n = scales.shape
    words = np.ascontiguousarray(words).reshape(g, 128, n, -1)
    if fmt == "e4m3":
        vals = words.view(ml_dtypes.float8_e4m3fn).astype(np.float64)
    else:
        nib = np.empty((g, 128, n, 4), np.uint8)
        nib[..., 0::2] = words & 0xF
        nib[..., 1::2] = words >> 4
        vals = E2M1[nib]
    vals = vals * np.repeat(np.exp2(scales.astype(np.float64) - 127.0), 8, axis=1)[..., None]
    return vals.transpose(0, 1, 3, 2).reshape(g * 512, n)


def sigmoid(v):
    return 1.0 / (1.0 + np.exp(-v))


D, E, T, I, Q = 512, 512, 2048, 512, 128


def setup_inputs():
    n = np.random.standard_normal
    idx = np.random.permutation(T)[:I]
    fd = mx_kscale(D)
    fe = mx_kscale(E)
    fi = mx_kscale(I)
    ti = np.ones(T)
    ti[idx] = fi
    keysp = pack_weight(n((D, T)) / fd[:, None], "e4m3")
    valsp = pack_weight(n((E, T)) / fe[:, None], "e4m3")
    return {
        "query": (n((D, Q)) * 0.5 / np.sqrt(D) * fd[:, None]).astype(np.float32),
        "query2": (n((D, Q)) * 0.6 / np.sqrt(D) * fd[:, None]).astype(np.float32),
        "keys_words": keysp[0],
        "keys_scales": keysp[1],
        "age": np.tile(np.random.uniform(0.0, 2.0, T), (128, 1)).astype(np.float32),
        "grace": (np.random.uniform(0.7, 1.5, (Q, 1))).astype(np.float32),
        "gout": (n((E, Q)) * 1 / np.sqrt(E) * fe[:, None]).astype(np.float32),
        "vals_words": valsp[0],
        "vals_scales": valsp[1],
        "size": (np.random.uniform(0.5, 2.0, (1, I))).astype(np.float32),
        "fs": (np.random.uniform(128.0, 512.0, (1, I)) * fi).astype(np.float32),
        "keyrows": (n((D, T)) / ti).astype(np.float32),
        "res": (n((Q, D)) * 4.0).astype(np.float32),
        "offs": striped(idx),
    }


def reference(query, query2, keys_words, keys_scales, age, grace, gout, vals_words, vals_scales, size, fs, keyrows, res, offs):
    idx = unstriped(offs)
    keysu = unpack_weight(keys_words, keys_scales, "e4m3")
    valsu = unpack_weight(vals_words, vals_scales, "e4m3")
    queryq = mxq(f64(query), 0, "e4m3")
    keysidxg = keysu[:, idx]
    a = queryq.T @ keysidxg
    query2q = mxq(f64(query2), 0, "e4m3")
    b = query2q.T @ keysidxg
    r = np.exp(a - np.max(a, axis=1, keepdims=True))
    gt = sigmoid((b + f64(grace) - f64(age)[:1][:, idx]) * 3.0)
    p = r * gt
    z = np.sum(p, axis=1, keepdims=True)
    goutq = mxq(f64(gout), 0, "e4m3")
    valsidxg = valsu[:, idx]
    c0 = goutq.T @ valsidxg
    dz = np.sum(c0 * p * f64(size) / np.square(z) * (-1.0), axis=1, keepdims=True)
    dp = c0 / z * f64(size) + dz
    dgt = dp * r
    db = dgt * gt * (1.0 - gt) * 3.0
    gs = db * f64(fs)
    gt1 = gs.T
    kt = f64(keyrows)[:, idx].T
    gt1q = mxq(gt1, 0, "e4m3")
    ktq = mxq(kt, 0, "e4m3")
    gq = gt1q.T @ ktq
    y = gq + f64(res)
    return y

@@ -1,0 +1,234 @@
+from contextlib import ExitStack
+
+import concourse.mybir as mybir
+
+D, E, T, I, Q = 512, 512, 2048, 512, 128
+FLOPS = 4 * 2 * 512 * 512 * 128
+
+F32 = mybir.dt.float32
+BF16 = mybir.dt.bfloat16
+I32 = mybir.dt.int32
+U32 = mybir.dt.uint32
+U16 = mybir.dt.uint16
+U8 = mybir.dt.uint8
+FP8X4 = mybir.dt.float8_e4m3fn_x4
+ALU = mybir.AluOpType
+ACT = mybir.ActivationFunctionType
+AXIS = mybir.AxisListType
+
+P = 128
+PACK = 4
+NB = 4
+
+
+def tile_attend_bsoftlives_b_q_kernel(tc, query, query2, keys_words, keys_scales, age, grace, gout,
+                                       vals_words, vals_scales, size, fs, keyrows, res, offs, out):
+    nc = tc.nc
+    with ExitStack() as ctx:
+        lists = ctx.enter_context(tc.tile_pool(name="lists", bufs=1))
+        early = ctx.enter_context(tc.tile_pool(name="early", bufs=1))
+        ps = ctx.enter_context(tc.psum_pool(name="ps", bufs=1))
+        ps2 = ctx.enter_context(tc.psum_pool(name="ps2", bufs=2))
+
+        offsets = lists.tile([P, I // 16], U16, name="offsets")
+        k_bytes = early.tile([P, T], U8, name="k_bytes")
+        v_bytes = early.tile([P, T], U8, name="v_bytes")
+        age_pool = early.tile([P, T], F32, name="age_pool")
+        rows = early.tile([P, P], F32, name="rows")
+        ident = early.tile([P, P], F32, name="ident")
+        q1_raw = early.tile([P, PACK, Q], F32, name="q1_raw")
+        half = P // 2
+
+        def identity_half(pool, tag, h):
+            diff = pool.tile([P, half], I32, tag=tag, name="diff%d" % h)
+            nc.gpsimd.iota(diff[:], pattern=[[-1, half]], base=-h * half, channel_multiplier=1)
+            nc.vector.tensor_scalar(out=ident[:, h * half:(h + 1) * half], in0=diff[:], scalar1=0.0, scalar2=None,
+                                    op0=ALU.is_equal)
+
+        nc.vector.memset(k_bytes[:].bitcast(I32), 0)
+        identity_half(early, "k_words", 0)
+        k_words = early.tile([P, T], U32, tag="k_words", name="k_words")
+        nc.vector.memset(age_pool[:], 0.0)
+        nc.vector.memset(v_bytes[:].bitcast(I32), 0)
+        nc.vector.memset(rows[:], 0.0)
+        with tc.tile_pool(name="scratch", bufs=1) as scratch:
+            identity_half(scratch, "diff", 1)
+
+        sb = ctx.enter_context(tc.tile_pool(name="sb", bufs=1))
+        q2_raw = sb.tile([P, PACK, Q], F32, name="q2_raw")
+        v_words = sb.tile([P, T], U32, name="v_words")
+        g_raw = sb.tile([P, PACK, Q], F32, name="g_raw")
+        fs_cols = sb.tile([P, PACK], F32, name="fs_cols")
+        res_sb = sb.tile([P, D], F32, name="res_sb")
+        kr = [sb.tile([P, T], F32, name="kr%d" % j) for j in range(NB)]
+
+        def load_bytes(queue, tile, scales):
+            for quad in range(4):
+                queue.dma_start(out=tile[32 * quad:32 * quad + 4, :].bitcast(I32),
+                                in_=scales[0, 4 * quad:4 * quad + 4, :].bitcast(I32))
+
+        def load_words(tile, words):
+            nc.sync.dma_start(out=tile[:].bitcast(I32), in_=words[0].rearrange("p n t -> p (n t)").bitcast(I32))
+
+        def load_operand(tile, src):
+            nc.sync.dma_start(out=tile[:], in_=src.rearrange("(p j) w -> p j w", j=PACK))
+
+        load_operand(q1_raw, query)
+        nc.sync.dma_start(offsets[:], offs)
+        load_bytes(nc.sync, k_bytes, keys_scales)
+        load_words(k_words, keys_words)
+        nc.scalar.dma_start(out=age_pool[0:1, :], in_=age[0:1, :])
+        load_operand(q2_raw, query2)
+        load_operand(g_raw, gout)
+        load_bytes(nc.sync, v_bytes, vals_scales)
+        load_words(v_words, vals_words)
+        nc.sync.dma_start(out=rows[NB:NB + 1, :], in_=grace.rearrange("q o -> o q"))
+        nc.sync.dma_start(out=rows[0:NB, :], in_=size.rearrange("o (j s) -> (o j) s", j=NB))
+        nc.sync.dma_start(out=fs_cols[:], in_=fs.rearrange("o (p t) -> (o p) t", t=PACK))
+        for j in range(NB):
+            nc.sync.dma_start(out=kr[j][:], in_=keyrows[j * P:(j + 1) * P, :])
+        nc.sync.dma_start(out=res_sb[:], in_=res)
+
+        def weave(grouped, raw):
+            nc.scalar.activation(out=grouped.rearrange("p (c i t) -> p c t i", i=4, t=PACK),
+                                 in_=raw[:].rearrange("p t (c i) -> p c t i", i=4), func=ACT.Copy)
+
+        def quantise(name, grouped, width):
+            codes = sb.tile([P, width], U32, name=name + "_codes", align_bytes=64)
+            scales = sb.tile([P, width], U8, name=name + "_scales", align_bytes=64)
+            nc.vector.quantize_mx(out=codes[:].bitcast(FP8X4), scales=scales[:], in_=grouped)
+            return codes, scales
+
+        def product(acc, lhs, lcols, rhs, rcols):
+            nc.tensor.matmul_mx(out=acc, lhsT=lhs[0][:, lcols].bitcast(FP8X4), lhsT_scale=lhs[1][:, lcols],
+                                rhs=rhs[0][:, rcols].bitcast(FP8X4), rhs_scale=rhs[1][:, rcols],
+                                start=True, stop=True)
+
+        def gather(name, window, dtype):
+            got = sb.tile([P, I], dtype, name=name, align_bytes=64)
+            nc.vector.tensor_copy(got[:], window[:].indirect(offsets[:]))
+            return got
+
+        def blk(j):
+            return slice(j * P, (j + 1) * P)
+
+        def dealt(bank):
+            return bank[:].rearrange("p (s t) -> p t s", t=PACK)
+
+        qq = sb.tile([P, 2 * Q * PACK], BF16, name="qq", align_bytes=64)
+        weave(qq[:, 0:Q * PACK], q1_raw)
+        weave(qq[:, Q * PACK:], q2_raw)
+        gg = sb.tile([P, Q * PACK], BF16, name="gg", align_bytes=64)
+        weave(gg[:], g_raw)
+        k_bytes_g = gather("k_bytes_g", k_bytes, U8)
+        age_g = gather("age_g", age_pool, F32)
+        keys = (gather("k_words_g", k_words, U32), k_bytes_g)
+        qq_mx = quantise("qq", qq[:], 2 * Q)
+
+        age_t = ps.tile([P, NB, P], F32, tag="m", name="age_t")
+        for j in range(NB):
+            nc.tensor.transpose(age_t[:, j, :], age_g[:, blk(j)], ident[:])
+        neg_age = sb.tile([P, NB], F32, name="neg_age")
+        nc.scalar.activation(out=neg_age[:], in_=age_t[:, :, 0], func=ACT.Copy, scale=-1.0)
+        rows_t = ps.tile([P, P], F32, tag="o", name="rows_t")
+        nc.tensor.transpose(rows_t[:], rows[:], ident[:])
+        size_cols = sb.tile([P, NB], F32, name="size_cols")
+        nc.scalar.activation(out=size_cols[:], in_=rows_t[:, 0:NB], func=ACT.Copy)
+        grace15 = sb.tile([P, 1], F32, name="grace15")
+        nc.scalar.activation(out=grace15[:], in_=rows_t[:, NB:NB + 1], func=ACT.Copy, scale=1.5)
+        fs15 = sb.tile([P, PACK], F32, name="fs15")
+        nc.scalar.activation(out=fs15[:], in_=fs_cols[:], func=ACT.Copy, scale=1.5)
+
+        b_t = ps.tile([P, NB, Q], F32, tag="T", name="b_t")
+        for j in range(NB):
+            product(b_t[:, j, :], keys, blk(j), qq_mx, slice(Q, 2 * Q))
+        a = ps.tile([P, I], F32, tag="a", name="a")
+        product(a[:], qq_mx, slice(0, Q), keys, slice(0, I))
+
+        v_bytes_g = gather("v_bytes_g", v_bytes, U8)
+        g_mx = quantise("g", gg[:], Q)
+        neg_max = sb.tile([P, 1], F32, name="neg_max")
+        nc.vector.tensor_reduce(out=neg_max[:], in_=a[:], axis=AXIS.X, op=ALU.max, negate=True)
+        vals = (gather("v_words_g", v_words, U32), v_bytes_g)
+
+        x_t = sb.tile([P, NB, Q], F32, name="x_t")
+        x = ps.tile([P, I], F32, tag="x", name="x")
+        for j in range(NB):
+            nc.scalar.activation(out=x_t[:, j, :], in_=b_t[:, j, :], func=ACT.Identity, bias=neg_age[:, j:j + 1])
+        for j in range(NB):
+            nc.tensor.transpose(x[:, blk(j)], x_t[:, j, :], ident[:])
+        th = sb.tile([P, PACK, P], F32, name="th")
+        nc.scalar.activation(out=th[:], in_=dealt(x), func=ACT.Tanh, bias=grace15[:], scale=1.5)
+        r = sb.tile([P, PACK, P], F32, name="r")
+        nc.scalar.activation(out=r[:], in_=dealt(a), func=ACT.Exp, bias=neg_max[:])
+
+        c_t = ps.tile([P, NB, Q], F32, tag="T", name="c_t")
+        for j in range(NB):
+            product(c_t[:, j, :], vals, blk(j), g_mx, slice(0, Q))
+        cs_t = sb.tile([P, NB, Q], F32, name="cs_t")
+        cs = ps.tile([P, I], F32, tag="cs", name="cs")
+        for j in range(NB):
+            nc.scalar.activation(out=cs_t[:, j, :], in_=c_t[:, j, :], func=ACT.Copy, scale=size_cols[:, j:j + 1])
+        for j in range(NB):
+            nc.tensor.transpose(cs[:, blk(j)], cs_t[:, j, :], ident[:])
+
+        def key_rows_gather(j):
+            return gather("kr_g%d" % j, kr[j], BF16)
+
+        def key_rows_turn(j, got):
+            words = got[:].bitcast(F32)
+            bank = ps2.tile([P, 2, P], F32, tag="k", name="kt_bank%d" % j)
+            for u in range(2):
+                nc.tensor.transpose(bank[:, u, :], words[:, u:I // 2:2], ident[:])
+            grouped = sb.tile([P, P * PACK], BF16, name="kt%d" % j, align_bytes=64)
+            nc.scalar.copy(out=grouped[:].bitcast(F32).rearrange("p (r u) -> p r u", u=2),
+                           in_=bank[:].rearrange("p u r -> p r u"))
+            return grouped
+
+        p2 = sb.tile([P, PACK, P], F32, name="p2")
+        z2 = sb.tile([P, 1], F32, name="z2")
+        nc.vector.scalar_tensor_tensor(out=p2[:], in0=th[:], scalar=1.0, in1=r[:], op0=ALU.add, op1=ALU.mult,
+                                       accum_out=z2[:])
+        rz = sb.tile([P, 1], F32, name="rz")
+        nc.vector.reciprocal(out=rz[:], in_=z2[:])
+        kt = [None] * NB
+        kt[0] = key_rows_turn(0, key_rows_gather(0))
+        e = sb.tile([P, PACK, P], F32, name="e")
+        m = sb.tile([P, 1], F32, name="m")
+        nc.vector.scalar_tensor_tensor(out=e[:], in0=dealt(cs), scalar=rz[:], in1=p2[:], op0=ALU.mult, op1=ALU.mult,
+                                       accum_out=m[:])
+        mz = sb.tile([P, 1], F32, name="mz")
+        nc.vector.tensor_tensor(out=mz[:], in0=m[:], in1=rz[:], op=ALU.mult)
+        f = sb.tile([P, PACK, P], F32, name="f")
+        nc.vector.scalar_tensor_tensor(out=f[:], in0=p2[:], scalar=mz[:], in1=e[:], op0=ALU.mult, op1=ALU.subtract)
+        db = sb.tile([P, PACK, P], F32, name="db")
+        nc.vector.scalar_tensor_tensor(out=db[:], in0=th[:], scalar=1.0, in1=f[:], op0=ALU.subtract, op1=ALU.mult)
+        db_t = ps.tile([P, PACK, Q], F32, tag="m", name="db_t")
+        for t in range(PACK):
+            nc.tensor.transpose(db_t[:, t, :], db[:, t, :], ident[:])
+        kt[1] = key_rows_turn(1, key_rows_gather(1))
+        gs = sb.tile([P, Q * PACK], BF16, name="gs", align_bytes=64)
+        nc.vector.tensor_tensor(out=gs[:].rearrange("p (q t) -> p q t", t=PACK), in0=db_t[:].rearrange("p t q -> p q t"),
+                                in1=fs15[:].unsqueeze(1).to_broadcast([P, Q, PACK]), op=ALU.mult)
+        kt_mx = [None] * NB
+        kt_mx[0] = quantise("kt0", kt[0][:], P)
+        gs_mx = quantise("gs", gs[:], Q)
+        kt[2] = key_rows_turn(2, key_rows_gather(2))
+        kt_mx[1] = quantise("kt1", kt[1][:], P)
+        kt[3] = key_rows_turn(3, key_rows_gather(3))
+        kt_mx[2] = quantise("kt2", kt[2][:], P)
+
+        head = (NB - 1) * P
+        gq_head = ps.tile([P, head], F32, tag="o", name="gq_head")
+        for j in range(NB - 1):
+            product(gq_head[:, blk(j)], gs_mx, slice(0, Q), kt_mx[j], slice(0, P))
+        y_head = sb.tile([P, head], F32, name="y_head")
+        nc.vector.tensor_tensor(out=y_head[:], in0=gq_head[:], in1=res_sb[:, 0:head], op=ALU.add)
+        nc.sync.dma_start(out=out[:, 0:head], in_=y_head[:])
+
+        kt_mx[3] = quantise("kt3", kt[3][:], P)
+        gq_tail = ps.tile([P, P], F32, tag="x", name="gq_tail")
+        product(gq_tail[:], gs_mx, slice(0, Q), kt_mx[3], slice(0, P))
+        y_tail = sb.tile([P, P], F32, name="y_tail")
+        nc.vector.tensor_tensor(out=y_tail[:], in0=gq_tail[:], in1=res_sb[:, head:D], op=ALU.add)
+        nc.sync.dma_start(out=out[:, head:D], in_=y_tail[:])

@@ -32,69 +32,76 @@ def tile_attend_bsoftlives_b_q_kernel(tc, query, query2, keys_words, keys_scales
 
         offsets = lists.tile([P, I // 16], U16, name="offsets")
         k_bytes = early.tile([P, T], U8, name="k_bytes")
-        v_bytes = early.tile([P, T], U8, name="v_bytes")
+        v_bytes = early.tile([P, T], U8, tag="v_bytes", name="v_bytes")
         age_pool = early.tile([P, T], F32, name="age_pool")
         rows = early.tile([P, P], F32, name="rows")
         ident = early.tile([P, P], F32, name="ident")
         q1_raw = early.tile([P, PACK, Q], F32, name="q1_raw")
-        half = P // 2
+        q2_raw = early.tile([P, PACK, Q], F32, name="q2_raw")
+        pieces = (0, 32, 64, 96, 128)
+        split = 1536
 
-        def identity_half(pool, tag, h):
-            diff = pool.tile([P, half], I32, tag=tag, name="diff%d" % h)
-            nc.gpsimd.iota(diff[:], pattern=[[-1, half]], base=-h * half, channel_multiplier=1)
-            nc.vector.tensor_scalar(out=ident[:, h * half:(h + 1) * half], in0=diff[:], scalar1=0.0, scalar2=None,
-                                    op0=ALU.is_equal)
+        def identity_piece(pool, tag, h):
+            lo, hi = pieces[h], pieces[h + 1]
+            zeros = pool.tile([P, hi - lo], F32, tag=tag, name="zeros%d" % h)
+            nc.gpsimd.memset(zeros[:], 0.0)
+            nc.gpsimd.affine_select(out=ident[:, lo:hi], in_=zeros[:], compare_op=ALU.not_equal,
+                                    fill=1.0, base=-lo, pattern=[[-1, hi - lo]], channel_multiplier=1)
 
-        nc.vector.memset(k_bytes[:].bitcast(I32), 0)
-        identity_half(early, "k_words", 0)
-        k_words = early.tile([P, T], U32, tag="k_words", name="k_words")
-        nc.vector.memset(age_pool[:], 0.0)
-        nc.vector.memset(v_bytes[:].bitcast(I32), 0)
-        nc.vector.memset(rows[:], 0.0)
         with tc.tile_pool(name="scratch", bufs=1) as scratch:
-            identity_half(scratch, "diff", 1)
+            nc.vector.memset(age_pool[:, 0:split - 1], 0.0)
+            nc.vector.memset(age_pool[:, split - 1:split], 0.0)
+            nc.gpsimd.memset(k_bytes[:].bitcast(I32), 0)
+            identity_piece(early, "k_words", 0)
+            nc.gpsimd.memset(age_pool[:, split:T], 0.0)
+            nc.gpsimd.memset(v_bytes[:].bitcast(I32), 0)
+            identity_piece(early, "g_raw", 1)
+            identity_piece(early, "v_words", 2)
+            nc.gpsimd.memset(rows[:], 0.0)
+            identity_piece(scratch, "zeros", 3)
 
+        k_words = early.tile([P, T], U32, tag="k_words", name="k_words")
+        g_raw = early.tile([P, PACK, Q], F32, tag="g_raw", name="g_raw")
+        v_words = early.tile([P, T], U32, tag="v_words", name="v_words")
         sb = ctx.enter_context(tc.tile_pool(name="sb", bufs=1))
-        q2_raw = sb.tile([P, PACK, Q], F32, name="q2_raw")
-        v_words = sb.tile([P, T], U32, name="v_words")
-        g_raw = sb.tile([P, PACK, Q], F32, name="g_raw")
         fs_cols = sb.tile([P, PACK], F32, name="fs_cols")
         res_sb = sb.tile([P, D], F32, name="res_sb")
-        kr = [sb.tile([P, T], F32, name="kr%d" % j) for j in range(NB)]
+        kr = [sb.tile([P, T], F32, tag="kr%d" % j, name="kr%d" % j, align_bytes=64) for j in range(NB)]
 
-        def load_bytes(queue, tile, scales):
+        def load_bytes(tile, scales):
             for quad in range(4):
-                queue.dma_start(out=tile[32 * quad:32 * quad + 4, :].bitcast(I32),
+                nc.sync.dma_start(out=tile[32 * quad:32 * quad + 4, :].bitcast(I32),
                                 in_=scales[0, 4 * quad:4 * quad + 4, :].bitcast(I32))
 
         def load_words(tile, words):
             nc.sync.dma_start(out=tile[:].bitcast(I32), in_=words[0].rearrange("p n t -> p (n t)").bitcast(I32))
 
         def load_operand(tile, src):
-            nc.sync.dma_start(out=tile[:], in_=src.rearrange("(p j) w -> p j w", j=PACK))
+            nc.sync.dma_start(out=tile, in_=src.rearrange("(p j) w -> p j w", j=PACK))
 
-        load_operand(q1_raw, query)
         nc.sync.dma_start(offsets[:], offs)
-        load_bytes(nc.sync, k_bytes, keys_scales)
+        load_operand(q1_raw[:], query)
+        load_operand(q2_raw[:], query2)
+        load_bytes(k_bytes, keys_scales)
         load_words(k_words, keys_words)
-        nc.scalar.dma_start(out=age_pool[0:1, :], in_=age[0:1, :])
-        load_operand(q2_raw, query2)
-        load_operand(g_raw, gout)
-        load_bytes(nc.sync, v_bytes, vals_scales)
+        nc.sync.dma_start(out=age_pool[0:1, :], in_=age[0:1, :])
+        load_bytes(v_bytes, vals_scales)
+        load_operand(g_raw[:], gout)
         load_words(v_words, vals_words)
         nc.sync.dma_start(out=rows[NB:NB + 1, :], in_=grace.rearrange("q o -> o q"))
         nc.sync.dma_start(out=rows[0:NB, :], in_=size.rearrange("o (j s) -> (o j) s", j=NB))
-        nc.sync.dma_start(out=fs_cols[:], in_=fs.rearrange("o (p t) -> (o p) t", t=PACK))
         for j in range(NB):
             nc.sync.dma_start(out=kr[j][:], in_=keyrows[j * P:(j + 1) * P, :])
+            if j == 0:
+                nc.sync.dma_start(out=fs_cols[:], in_=fs.rearrange("o (p t) -> (o p) t", t=PACK))
         nc.sync.dma_start(out=res_sb[:], in_=res)
 
         def weave(grouped, raw):
             nc.scalar.activation(out=grouped.rearrange("p (c i t) -> p c t i", i=4, t=PACK),
-                                 in_=raw[:].rearrange("p t (c i) -> p c t i", i=4), func=ACT.Copy)
+                                 in_=raw.rearrange("p t (c i) -> p c t i", i=4), func=ACT.Copy)
 
-        def quantise(name, grouped, width):
-            codes = sb.tile([P, width], U32, name=name + "_codes", align_bytes=64)
+        def quantise(name, grouped, width, tag=""):
+            codes = sb.tile([P, width], U32, tag=tag or name + "_codes", name=name + "_codes", align_bytes=64)
             scales = sb.tile([P, width], U8, name=name + "_scales", align_bytes=64)
             nc.vector.quantize_mx(out=codes[:].bitcast(FP8X4), scales=scales[:], in_=grouped)
             return codes, scales
@@ -104,8 +111,8 @@ def tile_attend_bsoftlives_b_q_kernel(tc, query, query2, keys_words, keys_scales
                                 rhs=rhs[0][:, rcols].bitcast(FP8X4), rhs_scale=rhs[1][:, rcols],
                                 start=True, stop=True)
 
-        def gather(name, window, dtype):
-            got = sb.tile([P, I], dtype, name=name, align_bytes=64)
+        def gather(name, window, dtype, tag=""):
+            got = sb.tile([P, I], dtype, tag=tag or name, name=name, align_bytes=64)
             nc.vector.tensor_copy(got[:], window[:].indirect(offsets[:]))
             return got
 
@@ -115,56 +122,61 @@ def tile_attend_bsoftlives_b_q_kernel(tc, query, query2, keys_words, keys_scales
         def dealt(bank):
             return bank[:].rearrange("p (s t) -> p t s", t=PACK)
 
-        qq = sb.tile([P, 2 * Q * PACK], BF16, name="qq", align_bytes=64)
-        weave(qq[:, 0:Q * PACK], q1_raw)
-        weave(qq[:, Q * PACK:], q2_raw)
-        gg = sb.tile([P, Q * PACK], BF16, name="gg", align_bytes=64)
-        weave(gg[:], g_raw)
-        k_bytes_g = gather("k_bytes_g", k_bytes, U8)
-        age_g = gather("age_g", age_pool, F32)
-        keys = (gather("k_words_g", k_words, U32), k_bytes_g)
-        qq_mx = quantise("qq", qq[:], 2 * Q)
+        def turn_add(bank, tiles, start, stop):
+            for j, tile in enumerate(tiles):
+                nc.tensor.matmul(bank[:, blk(j)], lhsT=tile, rhs=ident[:], is_transpose=True,
+                                 start=start and j == 0, stop=stop and j == len(tiles) - 1)
 
+        qq = early.tile([P, 2 * Q * PACK], BF16, name="qq", align_bytes=64)
+        for h, raw in enumerate((q1_raw, q2_raw)):
+            nc.vector.tensor_copy(
+                out=qq[:, h * Q * PACK:(h + 1) * Q * PACK].rearrange("p (c i t) -> p c t i", i=4, t=PACK),
+                in_=raw[:].rearrange("p t (c i) -> p c t i", i=4))
+        k_bytes_g = gather("k_bytes_g", k_bytes, U8)
+        qq_mx = quantise("qq", qq[:], 2 * Q)
+        keys = (gather("k_words_g", k_words, U32), k_bytes_g)
+        age_g = gather("age_g", age_pool, F32)
+
+        every = slice(0, Q)
+        b_t = ps.tile([P, NB, Q], F32, tag="T", name="b_t")
+        for j in range(NB):
+            product(b_t[:, j, :], keys, blk(j), qq_mx, slice(Q, 2 * Q))
+        a = ps.tile([P, I], F32, tag="a", name="a")
+        product(a[:], qq_mx, every, keys, slice(0, I))
+
+        g_w = sb.tile([P, Q * PACK], BF16, name="g_w", align_bytes=64)
+        weave(g_w[:], g_raw[:])
+        b_sb = sb.tile([P, NB, Q], F32, name="b_sb")
+        nc.scalar.activation(out=b_sb[:], in_=b_t[:], func=ACT.Copy)
         age_t = ps.tile([P, NB, P], F32, tag="m", name="age_t")
         for j in range(NB):
             nc.tensor.transpose(age_t[:, j, :], age_g[:, blk(j)], ident[:])
         neg_age = sb.tile([P, NB], F32, name="neg_age")
         nc.scalar.activation(out=neg_age[:], in_=age_t[:, :, 0], func=ACT.Copy, scale=-1.0)
-        rows_t = ps.tile([P, P], F32, tag="o", name="rows_t")
-        nc.tensor.transpose(rows_t[:], rows[:], ident[:])
-        size_cols = sb.tile([P, NB], F32, name="size_cols")
-        nc.scalar.activation(out=size_cols[:], in_=rows_t[:, 0:NB], func=ACT.Copy)
-        grace15 = sb.tile([P, 1], F32, name="grace15")
-        nc.scalar.activation(out=grace15[:], in_=rows_t[:, NB:NB + 1], func=ACT.Copy, scale=1.5)
-        fs15 = sb.tile([P, PACK], F32, name="fs15")
-        nc.scalar.activation(out=fs15[:], in_=fs_cols[:], func=ACT.Copy, scale=1.5)
-
-        b_t = ps.tile([P, NB, Q], F32, tag="T", name="b_t")
-        for j in range(NB):
-            product(b_t[:, j, :], keys, blk(j), qq_mx, slice(Q, 2 * Q))
-        a = ps.tile([P, I], F32, tag="a", name="a")
-        product(a[:], qq_mx, slice(0, Q), keys, slice(0, I))
+        x = ps.tile([P, I], F32, tag="x", name="x")
+        turn_add(x, [b_sb[:, j, :] for j in range(NB)], True, False)
+        turn_add(x, [neg_age[:, j:j + 1].to_broadcast([P, P]) for j in range(NB)], False, True)
 
         v_bytes_g = gather("v_bytes_g", v_bytes, U8)
-        g_mx = quantise("g", gg[:], Q)
-        neg_max = sb.tile([P, 1], F32, name="neg_max")
+        neg_max = early.tile([P, 1], F32, tag="v_bytes", name="neg_max")
         nc.vector.tensor_reduce(out=neg_max[:], in_=a[:], axis=AXIS.X, op=ALU.max, negate=True)
+        g_mx = quantise("g", g_w[:], Q)
         vals = (gather("v_words_g", v_words, U32), v_bytes_g)
 
-        x_t = sb.tile([P, NB, Q], F32, name="x_t")
-        x = ps.tile([P, I], F32, tag="x", name="x")
-        for j in range(NB):
-            nc.scalar.activation(out=x_t[:, j, :], in_=b_t[:, j, :], func=ACT.Identity, bias=neg_age[:, j:j + 1])
-        for j in range(NB):
-            nc.tensor.transpose(x[:, blk(j)], x_t[:, j, :], ident[:])
-        th = sb.tile([P, PACK, P], F32, name="th")
-        nc.scalar.activation(out=th[:], in_=dealt(x), func=ACT.Tanh, bias=grace15[:], scale=1.5)
         r = sb.tile([P, PACK, P], F32, name="r")
         nc.scalar.activation(out=r[:], in_=dealt(a), func=ACT.Exp, bias=neg_max[:])
+        rows_t = ps.tile([P, P], F32, tag="T", name="rows_t")
+        nc.tensor.transpose(rows_t[:], rows[:], ident[:])
+        grace15 = sb.tile([P, 1], F32, name="grace15")
+        nc.scalar.activation(out=grace15[:], in_=rows_t[:, NB:NB + 1], func=ACT.Copy, scale=1.5)
+        size_cols = sb.tile([P, NB], F32, name="size_cols")
+        nc.scalar.activation(out=size_cols[:], in_=rows_t[:, 0:NB], func=ACT.Copy)
+        th = sb.tile([P, PACK, P], F32, name="th")
+        nc.scalar.activation(out=th[:], in_=dealt(x), func=ACT.Tanh, bias=grace15[:], scale=1.5)
 
         c_t = ps.tile([P, NB, Q], F32, tag="T", name="c_t")
         for j in range(NB):
-            product(c_t[:, j, :], vals, blk(j), g_mx, slice(0, Q))
+            product(c_t[:, j, :], vals, blk(j), g_mx, every)
         cs_t = sb.tile([P, NB, Q], F32, name="cs_t")
         cs = ps.tile([P, I], F32, tag="cs", name="cs")
         for j in range(NB):
@@ -172,63 +184,69 @@ def tile_attend_bsoftlives_b_q_kernel(tc, query, query2, keys_words, keys_scales
         for j in range(NB):
             nc.tensor.transpose(cs[:, blk(j)], cs_t[:, j, :], ident[:])
 
-        def key_rows_gather(j):
-            return gather("kr_g%d" % j, kr[j], BF16)
+        th_t = ps.tile([P, PACK, Q], F32, tag="T", name="th_t")
+        for t in range(PACK):
+            nc.tensor.transpose(th_t[:, t, :], th[:, t, :], ident[:])
+        fs_pos = sb.tile([P, PACK], F32, name="fs_pos")
+        nc.scalar.activation(out=fs_pos[:], in_=fs_cols[:], func=ACT.Copy, scale=1.5)
+        fs_neg = sb.tile([P, PACK], F32, name="fs_neg")
+        nc.scalar.activation(out=fs_neg[:], in_=fs_cols[:], func=ACT.Copy, scale=-1.5)
+        v_t = sb.tile([P, PACK, Q], F32, name="v_t")
+        for t in range(PACK):
+            nc.scalar.activation(out=v_t[:, t, :], in_=th_t[:, t, :], func=ACT.Identity, scale=fs_neg[:, t:t + 1],
+                                 bias=fs_pos[:, t:t + 1])
+        v_w = sb.tile([P, Q * PACK], F32, tag="v_w", name="v_w", align_bytes=64)
+        weave(v_w[:], v_t[:])
 
-        def key_rows_turn(j, got):
-            words = got[:].bitcast(F32)
+        def key_rows_turned(j, grouped):
+            words = gather("kr_g%d" % j, kr[j], BF16)[:].bitcast(F32)
             bank = ps2.tile([P, 2, P], F32, tag="k", name="kt_bank%d" % j)
             for u in range(2):
                 nc.tensor.transpose(bank[:, u, :], words[:, u:I // 2:2], ident[:])
-            grouped = sb.tile([P, P * PACK], BF16, name="kt%d" % j, align_bytes=64)
-            nc.scalar.copy(out=grouped[:].bitcast(F32).rearrange("p (r u) -> p r u", u=2),
+            nc.scalar.copy(out=grouped.bitcast(F32).rearrange("p (r u) -> p r u", u=2),
                            in_=bank[:].rearrange("p u r -> p r u"))
-            return grouped
 
-        p2 = sb.tile([P, PACK, P], F32, name="p2")
+        kt01 = sb.tile([P, 2 * P * PACK], BF16, name="kt01", align_bytes=64)
+        kt2 = sb.tile([P, P * PACK], BF16, name="kt2", align_bytes=64)
+        kt3 = sb.tile([P, P * PACK], BF16, name="kt3", align_bytes=64)
+        key_rows_turned(0, kt01[:, 0:P * PACK])
+        p2 = sb.tile([P, PACK, P], F32, tag="kr0", name="p2", align_bytes=64)
         z2 = sb.tile([P, 1], F32, name="z2")
         nc.vector.scalar_tensor_tensor(out=p2[:], in0=th[:], scalar=1.0, in1=r[:], op0=ALU.add, op1=ALU.mult,
                                        accum_out=z2[:])
         rz = sb.tile([P, 1], F32, name="rz")
         nc.vector.reciprocal(out=rz[:], in_=z2[:])
-        kt = [None] * NB
-        kt[0] = key_rows_turn(0, key_rows_gather(0))
-        e = sb.tile([P, PACK, P], F32, name="e")
+        neg_rz = sb.tile([P, 1], F32, name="neg_rz")
+        nc.scalar.activation(out=neg_rz[:], in_=rz[:], func=ACT.Copy, scale=-1.0)
+        key_rows_turned(1, kt01[:, P * PACK:])
+        e = sb.tile([P, PACK, P], F32, tag="kr1", name="e", align_bytes=64)
         m = sb.tile([P, 1], F32, name="m")
         nc.vector.scalar_tensor_tensor(out=e[:], in0=dealt(cs), scalar=rz[:], in1=p2[:], op0=ALU.mult, op1=ALU.mult,
                                        accum_out=m[:])
-        mz = sb.tile([P, 1], F32, name="mz")
-        nc.vector.tensor_tensor(out=mz[:], in0=m[:], in1=rz[:], op=ALU.mult)
-        f = sb.tile([P, PACK, P], F32, name="f")
-        nc.vector.scalar_tensor_tensor(out=f[:], in0=p2[:], scalar=mz[:], in1=e[:], op0=ALU.mult, op1=ALU.subtract)
-        db = sb.tile([P, PACK, P], F32, name="db")
-        nc.vector.scalar_tensor_tensor(out=db[:], in0=th[:], scalar=1.0, in1=f[:], op0=ALU.subtract, op1=ALU.mult)
-        db_t = ps.tile([P, PACK, Q], F32, tag="m", name="db_t")
-        for t in range(PACK):
-            nc.tensor.transpose(db_t[:, t, :], db[:, t, :], ident[:])
-        kt[1] = key_rows_turn(1, key_rows_gather(1))
-        gs = sb.tile([P, Q * PACK], BF16, name="gs", align_bytes=64)
-        nc.vector.tensor_tensor(out=gs[:].rearrange("p (q t) -> p q t", t=PACK), in0=db_t[:].rearrange("p t q -> p q t"),
-                                in1=fs15[:].unsqueeze(1).to_broadcast([P, Q, PACK]), op=ALU.mult)
-        kt_mx = [None] * NB
-        kt_mx[0] = quantise("kt0", kt[0][:], P)
+        neg_mz = sb.tile([P, 1], F32, name="neg_mz")
+        nc.scalar.activation(out=neg_mz[:], in_=m[:], func=ACT.Copy, scale=neg_rz[:])
+        u = sb.tile([P, PACK, P], F32, name="u")
+        nc.scalar.activation(out=u[:], in_=p2[:], func=ACT.Copy, scale=neg_mz[:])
+        f_t = ps.tile([P, PACK * Q], F32, tag="m", name="f_t")
+        turn_add(f_t, [e[:, t, :] for t in range(PACK)], True, False)
+        turn_add(f_t, [u[:, t, :] for t in range(PACK)], False, True)
+        key_rows_turned(2, kt2[:])
+        kt01_mx = quantise("kt01", kt01[:], 2 * P, tag="kr2")
+        key_rows_turned(3, kt3[:])
+        gs = sb.tile([P, Q * PACK], BF16, tag="kr3", name="gs", align_bytes=64)
+        nc.vector.tensor_tensor(out=gs[:].rearrange("p (q t) -> p q t", t=PACK), in0=f_t[:].rearrange("p (t q) -> p q t", t=PACK),
+                                in1=v_w[:].rearrange("p (q t) -> p q t", t=PACK), op=ALU.mult)
+        kt2_mx = quantise("kt2", kt2[:], P, tag="v_w")
         gs_mx = quantise("gs", gs[:], Q)
-        kt[2] = key_rows_turn(2, key_rows_gather(2))
-        kt_mx[1] = quantise("kt1", kt[1][:], P)
-        kt[3] = key_rows_turn(3, key_rows_gather(3))
-        kt_mx[2] = quantise("kt2", kt[2][:], P)
+        kt3_mx = quantise("kt3", kt3[:], P)
 
-        head = (NB - 1) * P
-        gq_head = ps.tile([P, head], F32, tag="o", name="gq_head")
-        for j in range(NB - 1):
-            product(gq_head[:, blk(j)], gs_mx, slice(0, Q), kt_mx[j], slice(0, P))
-        y_head = sb.tile([P, head], F32, name="y_head")
-        nc.vector.tensor_tensor(out=y_head[:], in0=gq_head[:], in1=res_sb[:, 0:head], op=ALU.add)
-        nc.sync.dma_start(out=out[:, 0:head], in_=y_head[:])
-
-        kt_mx[3] = quantise("kt3", kt[3][:], P)
-        gq_tail = ps.tile([P, P], F32, tag="x", name="gq_tail")
-        product(gq_tail[:], gs_mx, slice(0, Q), kt_mx[3], slice(0, P))
-        y_tail = sb.tile([P, P], F32, name="y_tail")
-        nc.vector.tensor_tensor(out=y_tail[:], in0=gq_tail[:], in1=res_sb[:, head:D], op=ALU.add)
-        nc.sync.dma_start(out=out[:, head:D], in_=y_tail[:])
+        half = D // 2
+        gq_lo = ps.tile([P, half], F32, tag="o", name="gq_lo")
+        product(gq_lo[:], gs_mx, every, kt01_mx, slice(0, half))
+        gq_hi = ps.tile([P, half], F32, tag="x", name="gq_hi")
+        product(gq_hi[:, blk(0)], gs_mx, every, kt2_mx, every)
+        product(gq_hi[:, blk(1)], gs_mx, every, kt3_mx, every)
+        for name, bank, cols in (("y_lo", gq_lo, slice(0, half)), ("y_hi", gq_hi, slice(half, D))):
+            y = sb.tile([P, half], F32, name=name)
+            nc.vector.tensor_tensor(out=y[:], in0=bank[:], in1=res_sb[:, cols], op=ALU.add)
+            nc.sync.dma_start(out=out[:, cols], in_=y[:])

from contextlib import ExitStack

import concourse.mybir as mybir

D, E, T, I, Q = 512, 512, 2048, 512, 128
FLOPS = 4 * 2 * 512 * 512 * 128

F32 = mybir.dt.float32
BF16 = mybir.dt.bfloat16
I32 = mybir.dt.int32
U32 = mybir.dt.uint32
U16 = mybir.dt.uint16
U8 = mybir.dt.uint8
FP8X4 = mybir.dt.float8_e4m3fn_x4
ALU = mybir.AluOpType
ACT = mybir.ActivationFunctionType
AXIS = mybir.AxisListType

P = 128
PACK = 4
NB = 4


def tile_attend_bsoftlives_b_q_kernel(tc, query, query2, keys_words, keys_scales, age, grace, gout,
                                       vals_words, vals_scales, size, fs, keyrows, res, offs, out):
    nc = tc.nc
    with ExitStack() as ctx:
        lists = ctx.enter_context(tc.tile_pool(name="lists", bufs=1))
        early = ctx.enter_context(tc.tile_pool(name="early", bufs=1))
        ps = ctx.enter_context(tc.psum_pool(name="ps", bufs=1))
        ps2 = ctx.enter_context(tc.psum_pool(name="ps2", bufs=2))

        offsets = lists.tile([P, I // 16], U16, name="offsets")
        k_bytes = early.tile([P, T], U8, name="k_bytes")
        v_bytes = early.tile([P, T], U8, tag="v_bytes", name="v_bytes")
        age_pool = early.tile([P, T], F32, name="age_pool")
        rows = early.tile([P, P], F32, name="rows")
        ident = early.tile([P, P], F32, name="ident")
        q1_raw = early.tile([P, PACK, Q], F32, name="q1_raw")
        q2_raw = early.tile([P, PACK, Q], F32, name="q2_raw")
        pieces = (0, 32, 64, 96, 128)
        split = 1536

        def identity_piece(pool, tag, h):
            lo, hi = pieces[h], pieces[h + 1]
            zeros = pool.tile([P, hi - lo], F32, tag=tag, name="zeros%d" % h)
            nc.gpsimd.memset(zeros[:], 0.0)
            nc.gpsimd.affine_select(out=ident[:, lo:hi], in_=zeros[:], compare_op=ALU.not_equal,
                                    fill=1.0, base=-lo, pattern=[[-1, hi - lo]], channel_multiplier=1)

        with tc.tile_pool(name="scratch", bufs=1) as scratch:
            nc.vector.memset(age_pool[:, 0:split - 1], 0.0)
            nc.vector.memset(age_pool[:, split - 1:split], 0.0)
            nc.gpsimd.memset(k_bytes[:].bitcast(I32), 0)
            identity_piece(early, "k_words", 0)
            nc.gpsimd.memset(age_pool[:, split:T], 0.0)
            nc.gpsimd.memset(v_bytes[:].bitcast(I32), 0)
            identity_piece(early, "g_raw", 1)
            identity_piece(early, "v_words", 2)
            nc.gpsimd.memset(rows[:], 0.0)
            identity_piece(scratch, "zeros", 3)

        k_words = early.tile([P, T], U32, tag="k_words", name="k_words")
        g_raw = early.tile([P, PACK, Q], F32, tag="g_raw", name="g_raw")
        v_words = early.tile([P, T], U32, tag="v_words", name="v_words")
        sb = ctx.enter_context(tc.tile_pool(name="sb", bufs=1))
        fs_cols = sb.tile([P, PACK], F32, name="fs_cols")
        res_sb = sb.tile([P, D], F32, name="res_sb")
        kr = [sb.tile([P, T], F32, tag="kr%d" % j, name="kr%d" % j, align_bytes=64) for j in range(NB)]

        def load_bytes(tile, scales):
            for quad in range(4):
                nc.sync.dma_start(out=tile[32 * quad:32 * quad + 4, :].bitcast(I32),
                                in_=scales[0, 4 * quad:4 * quad + 4, :].bitcast(I32))

        def load_words(tile, words):
            nc.sync.dma_start(out=tile[:].bitcast(I32), in_=words[0].rearrange("p n t -> p (n t)").bitcast(I32))

        def load_operand(tile, src):
            nc.sync.dma_start(out=tile, in_=src.rearrange("(p j) w -> p j w", j=PACK))

        nc.sync.dma_start(offsets[:], offs)
        load_operand(q1_raw[:], query)
        load_operand(q2_raw[:], query2)
        load_bytes(k_bytes, keys_scales)
        load_words(k_words, keys_words)
        nc.sync.dma_start(out=age_pool[0:1, :], in_=age[0:1, :])
        load_bytes(v_bytes, vals_scales)
        load_operand(g_raw[:], gout)
        load_words(v_words, vals_words)
        nc.sync.dma_start(out=rows[NB:NB + 1, :], in_=grace.rearrange("q o -> o q"))
        nc.sync.dma_start(out=rows[0:NB, :], in_=size.rearrange("o (j s) -> (o j) s", j=NB))
        for j in range(NB):
            nc.sync.dma_start(out=kr[j][:], in_=keyrows[j * P:(j + 1) * P, :])
            if j == 0:
                nc.sync.dma_start(out=fs_cols[:], in_=fs.rearrange("o (p t) -> (o p) t", t=PACK))
        nc.sync.dma_start(out=res_sb[:], in_=res)

        def weave(grouped, raw):
            nc.scalar.activation(out=grouped.rearrange("p (c i t) -> p c t i", i=4, t=PACK),
                                 in_=raw.rearrange("p t (c i) -> p c t i", i=4), func=ACT.Copy)

        def quantise(name, grouped, width, tag=""):
            codes = sb.tile([P, width], U32, tag=tag or name + "_codes", name=name + "_codes", align_bytes=64)
            scales = sb.tile([P, width], U8, name=name + "_scales", align_bytes=64)
            nc.vector.quantize_mx(out=codes[:].bitcast(FP8X4), scales=scales[:], in_=grouped)
            return codes, scales

        def product(acc, lhs, lcols, rhs, rcols):
            nc.tensor.matmul_mx(out=acc, lhsT=lhs[0][:, lcols].bitcast(FP8X4), lhsT_scale=lhs[1][:, lcols],
                                rhs=rhs[0][:, rcols].bitcast(FP8X4), rhs_scale=rhs[1][:, rcols],
                                start=True, stop=True)

        def gather(name, window, dtype, tag=""):
            got = sb.tile([P, I], dtype, tag=tag or name, name=name, align_bytes=64)
            nc.vector.tensor_copy(got[:], window[:].indirect(offsets[:]))
            return got

        def blk(j):
            return slice(j * P, (j + 1) * P)

        def dealt(bank):
            return bank[:].rearrange("p (s t) -> p t s", t=PACK)

        def turn_add(bank, tiles, start, stop):
            for j, tile in enumerate(tiles):
                nc.tensor.matmul(bank[:, blk(j)], lhsT=tile, rhs=ident[:], is_transpose=True,
                                 start=start and j == 0, stop=stop and j == len(tiles) - 1)

        qq = early.tile([P, 2 * Q * PACK], BF16, name="qq", align_bytes=64)
        for h, raw in enumerate((q1_raw, q2_raw)):
            nc.vector.tensor_copy(
                out=qq[:, h * Q * PACK:(h + 1) * Q * PACK].rearrange("p (c i t) -> p c t i", i=4, t=PACK),
                in_=raw[:].rearrange("p t (c i) -> p c t i", i=4))
        k_bytes_g = gather("k_bytes_g", k_bytes, U8)
        qq_mx = quantise("qq", qq[:], 2 * Q)
        keys = (gather("k_words_g", k_words, U32), k_bytes_g)
        age_g = gather("age_g", age_pool, F32)

        every = slice(0, Q)
        b_t = ps.tile([P, NB, Q], F32, tag="T", name="b_t")
        for j in range(NB):
            product(b_t[:, j, :], keys, blk(j), qq_mx, slice(Q, 2 * Q))
        a = ps.tile([P, I], F32, tag="a", name="a")
        product(a[:], qq_mx, every, keys, slice(0, I))

        g_w = sb.tile([P, Q * PACK], BF16, name="g_w", align_bytes=64)
        weave(g_w[:], g_raw[:])
        b_sb = sb.tile([P, NB, Q], F32, name="b_sb")
        nc.scalar.activation(out=b_sb[:], in_=b_t[:], func=ACT.Copy)
        age_t = ps.tile([P, NB, P], F32, tag="m", name="age_t")
        for j in range(NB):
            nc.tensor.transpose(age_t[:, j, :], age_g[:, blk(j)], ident[:])
        neg_age = sb.tile([P, NB], F32, name="neg_age")
        nc.scalar.activation(out=neg_age[:], in_=age_t[:, :, 0], func=ACT.Copy, scale=-1.0)
        x = ps.tile([P, I], F32, tag="x", name="x")
        turn_add(x, [b_sb[:, j, :] for j in range(NB)], True, False)
        turn_add(x, [neg_age[:, j:j + 1].to_broadcast([P, P]) for j in range(NB)], False, True)

        v_bytes_g = gather("v_bytes_g", v_bytes, U8)
        neg_max = early.tile([P, 1], F32, tag="v_bytes", name="neg_max")
        nc.vector.tensor_reduce(out=neg_max[:], in_=a[:], axis=AXIS.X, op=ALU.max, negate=True)
        g_mx = quantise("g", g_w[:], Q)
        vals = (gather("v_words_g", v_words, U32), v_bytes_g)

        r = sb.tile([P, PACK, P], F32, name="r")
        nc.scalar.activation(out=r[:], in_=dealt(a), func=ACT.Exp, bias=neg_max[:])
        rows_t = ps.tile([P, P], F32, tag="T", name="rows_t")
        nc.tensor.transpose(rows_t[:], rows[:], ident[:])
        grace15 = sb.tile([P, 1], F32, name="grace15")
        nc.scalar.activation(out=grace15[:], in_=rows_t[:, NB:NB + 1], func=ACT.Copy, scale=1.5)
        size_cols = sb.tile([P, NB], F32, name="size_cols")
        nc.scalar.activation(out=size_cols[:], in_=rows_t[:, 0:NB], func=ACT.Copy)
        th = sb.tile([P, PACK, P], F32, name="th")
        nc.scalar.activation(out=th[:], in_=dealt(x), func=ACT.Tanh, bias=grace15[:], scale=1.5)

        c_t = ps.tile([P, NB, Q], F32, tag="T", name="c_t")
        for j in range(NB):
            product(c_t[:, j, :], vals, blk(j), g_mx, every)
        cs_t = sb.tile([P, NB, Q], F32, name="cs_t")
        cs = ps.tile([P, I], F32, tag="cs", name="cs")
        for j in range(NB):
            nc.scalar.activation(out=cs_t[:, j, :], in_=c_t[:, j, :], func=ACT.Copy, scale=size_cols[:, j:j + 1])
        for j in range(NB):
            nc.tensor.transpose(cs[:, blk(j)], cs_t[:, j, :], ident[:])

        th_t = ps.tile([P, PACK, Q], F32, tag="T", name="th_t")
        for t in range(PACK):
            nc.tensor.transpose(th_t[:, t, :], th[:, t, :], ident[:])
        fs_pos = sb.tile([P, PACK], F32, name="fs_pos")
        nc.scalar.activation(out=fs_pos[:], in_=fs_cols[:], func=ACT.Copy, scale=1.5)
        fs_neg = sb.tile([P, PACK], F32, name="fs_neg")
        nc.scalar.activation(out=fs_neg[:], in_=fs_cols[:], func=ACT.Copy, scale=-1.5)
        v_t = sb.tile([P, PACK, Q], F32, name="v_t")
        for t in range(PACK):
            nc.scalar.activation(out=v_t[:, t, :], in_=th_t[:, t, :], func=ACT.Identity, scale=fs_neg[:, t:t + 1],
                                 bias=fs_pos[:, t:t + 1])
        v_w = sb.tile([P, Q * PACK], F32, tag="v_w", name="v_w", align_bytes=64)
        weave(v_w[:], v_t[:])

        def key_rows_turned(j, grouped):
            words = gather("kr_g%d" % j, kr[j], BF16)[:].bitcast(F32)
            bank = ps2.tile([P, 2, P], F32, tag="k", name="kt_bank%d" % j)
            for u in range(2):
                nc.tensor.transpose(bank[:, u, :], words[:, u:I // 2:2], ident[:])
            nc.scalar.copy(out=grouped.bitcast(F32).rearrange("p (r u) -> p r u", u=2),
                           in_=bank[:].rearrange("p u r -> p r u"))

        kt01 = sb.tile([P, 2 * P * PACK], BF16, name="kt01", align_bytes=64)
        kt2 = sb.tile([P, P * PACK], BF16, name="kt2", align_bytes=64)
        kt3 = sb.tile([P, P * PACK], BF16, name="kt3", align_bytes=64)
        key_rows_turned(0, kt01[:, 0:P * PACK])
        p2 = sb.tile([P, PACK, P], F32, tag="kr0", name="p2", align_bytes=64)
        z2 = sb.tile([P, 1], F32, name="z2")
        nc.vector.scalar_tensor_tensor(out=p2[:], in0=th[:], scalar=1.0, in1=r[:], op0=ALU.add, op1=ALU.mult,
                                       accum_out=z2[:])
        rz = sb.tile([P, 1], F32, name="rz")
        nc.vector.reciprocal(out=rz[:], in_=z2[:])
        neg_rz = sb.tile([P, 1], F32, name="neg_rz")
        nc.scalar.activation(out=neg_rz[:], in_=rz[:], func=ACT.Copy, scale=-1.0)
        key_rows_turned(1, kt01[:, P * PACK:])
        e = sb.tile([P, PACK, P], F32, tag="kr1", name="e", align_bytes=64)
        m = sb.tile([P, 1], F32, name="m")
        nc.vector.scalar_tensor_tensor(out=e[:], in0=dealt(cs), scalar=rz[:], in1=p2[:], op0=ALU.mult, op1=ALU.mult,
                                       accum_out=m[:])
        neg_mz = sb.tile([P, 1], F32, name="neg_mz")
        nc.scalar.activation(out=neg_mz[:], in_=m[:], func=ACT.Copy, scale=neg_rz[:])
        u = sb.tile([P, PACK, P], F32, name="u")
        nc.scalar.activation(out=u[:], in_=p2[:], func=ACT.Copy, scale=neg_mz[:])
        f_t = ps.tile([P, PACK * Q], F32, tag="m", name="f_t")
        turn_add(f_t, [e[:, t, :] for t in range(PACK)], True, False)
        turn_add(f_t, [u[:, t, :] for t in range(PACK)], False, True)
        key_rows_turned(2, kt2[:])
        kt01_mx = quantise("kt01", kt01[:], 2 * P, tag="kr2")
        key_rows_turned(3, kt3[:])
        gs = sb.tile([P, Q * PACK], BF16, tag="kr3", name="gs", align_bytes=64)
        nc.vector.tensor_tensor(out=gs[:].rearrange("p (q t) -> p q t", t=PACK), in0=f_t[:].rearrange("p (t q) -> p q t", t=PACK),
                                in1=v_w[:].rearrange("p (q t) -> p q t", t=PACK), op=ALU.mult)
        kt2_mx = quantise("kt2", kt2[:], P, tag="v_w")
        gs_mx = quantise("gs", gs[:], Q)
        kt3_mx = quantise("kt3", kt3[:], P)

        half = D // 2
        gq_lo = ps.tile([P, half], F32, tag="o", name="gq_lo")
        product(gq_lo[:], gs_mx, every, kt01_mx, slice(0, half))
        gq_hi = ps.tile([P, half], F32, tag="x", name="gq_hi")
        product(gq_hi[:, blk(0)], gs_mx, every, kt2_mx, every)
        product(gq_hi[:, blk(1)], gs_mx, every, kt3_mx, every)
        for name, bank, cols in (("y_lo", gq_lo, slice(0, half)), ("y_hi", gq_hi, slice(half, D))):
            y = sb.tile([P, half], F32, name=name)
            nc.vector.tensor_tensor(out=y[:], in0=bank[:], in1=res_sb[:, cols], op=ALU.add)
            nc.sync.dma_start(out=out[:, cols], in_=y[:])
